import numpy as np
import ml_dtypes


def mxq(x, axis, fmt="e4m3"):
    dtype, down = {"e4m3": (ml_dtypes.float8_e4m3fn, 7), "e5m2": (ml_dtypes.float8_e5m2, 14)}[fmt]
    v = np.moveaxis(np.asarray(x, np.float32).astype(ml_dtypes.bfloat16).astype(np.float64), axis, -1)
    blocks = v.reshape(v.shape[:-1] + (-1, 32))
    amax = np.abs(blocks).max(-1, keepdims=True)
    byte = np.maximum(np.where(amax > 0, np.frexp(amax)[1] - 1 + 127, 0) - down, 1)
    scale = np.exp2(byte - 127.0)
    codes = (blocks / scale).astype(np.float32).astype(dtype).astype(np.float64)
    return np.moveaxis((codes * scale).reshape(v.shape), -1, axis)


WIDE = False


def mx_kscale(k):
    if not WIDE:
        return np.ones(k)
    levels = np.array([10, -10, 5, -5, 0])
    if k % 512:
        return np.exp2(np.random.permutation(np.resize(levels, k // 32))).repeat(32)
    a = np.empty((k // 512, 16))
    for p in range(k // 512):
        a[p, :8] = np.random.permutation(np.resize(levels, 8))
        for g in range(8):
            far = levels[np.abs(levels - a[p, g]) >= 10]
            a[p, g + 8] = far[np.random.randint(len(far))]
    return np.exp2(a.ravel()).repeat(32)


def f64(x):
    return np.asarray(x).astype(np.float64)


def striped(idx):
    return np.tile(np.asarray(idx).reshape(-1, 16).T, (8, 1)).astype(np.uint16)


def unstriped(offs):
    return offs[:16].T.reshape(-1).astype(np.int64)


E2M1 = np.array([0.0, 0.5, 1.0, 1.5, 2.0, 3.0, 4.0, 6.0, -0.0, -0.5, -1.0, -1.5, -2.0, -3.0, -4.0, -6.0])


def pack_weight(w, fmt):
    k, n = w.shape
    w = f64(np.asarray(w, np.float32).astype(ml_dtypes.bfloat16)).reshape(k // 32, 32, n)
    amax = np.abs(w).max(1)
    if fmt == "e4m3":
        byte = np.frexp(amax)[1] - 1 + 127 - 7
    else:
        mant, ex = np.frexp(amax / 6.0)
        byte = np.where(mant > 0.5, ex, ex - 1) + 127
    byte = np.clip(np.where(amax > 0, byte, 1), 1, 254)
    scaled = (w * np.exp2(127.0 - byte)[:, None, :]).reshape(k, n).astype(np.float32)
    by_word = np.ascontiguousarray(scaled.reshape(k // 512, 128, 4, n).transpose(0, 1, 3, 2))
    if fmt == "e4m3":
        words = by_word.astype(ml_dtypes.float8_e4m3fn).view(np.uint8)
    else:
        c = by_word.astype(ml_dtypes.float4_e2m1fn).view(np.uint8) & 0xF
        words = (c[..., 0::2] | (c[..., 1::2] << 4)).reshape(k // 512, 128, 2 * n)
    return np.ascontiguousarray(words), np.ascontiguousarray(byte.astype(np.uint8).reshape(k // 512, 16, n))


def unpack_weight(words, scales, fmt):
    g, _, n = scales.shape
    words = np.ascontiguousarray(words).reshape(g, 128, n, -1)
    if fmt == "e4m3":
        vals = words.view(ml_dtypes.float8_e4m3fn).astype(np.float64)
    else:
        nib = np.empty((g, 128, n, 4), np.uint8)
        nib[..., 0::2] = words & 0xF
        nib[..., 1::2] = words >> 4
        vals = E2M1[nib]
    vals = vals * np.repeat(np.exp2(scales.astype(np.float64) - 127.0), 8, axis=1)[..., None]
    return vals.transpose(0, 1, 3, 2).reshape(g * 512, n)


D, E, T, I, Q, G = 512, 512, 2048, 512, 128, 64


def setup_inputs():
    n = np.random.standard_normal
    idx = np.random.permutation(T)[:I]
    fd = mx_kscale(D)
    fe = mx_kscale(E)
    keysp = pack_weight(n((D, T)) / fd[:, None], "e2m1")
    valsp = pack_weight(n((E, T)) / fe[:, None], "e2m1")
    return {
        "query": (n((D, Q)) * 0.8 / np.sqrt(D) * fd[:, None]).astype(np.float32),
        "keys_words": keysp[0],
        "keys_scales": keysp[1],
        "mix": (np.random.uniform(0.2, 0.8, (Q, 1))).astype(np.float32),
        "gout": (n((E, Q)) * 1 / np.sqrt(E) * fe[:, None]).astype(np.float32),
        "vals_words": valsp[0],
        "vals_scales": valsp[1],
        "dquery": (n((D, Q)) * 1.0 / np.sqrt(D) * fd[:, None]).astype(np.float32),
        "base": (0.5 * n((Q, T))).astype(np.float32),
        "offs": striped(idx),
    }


def reference(query, keys_words, keys_scales, mix, gout, vals_words, vals_scales, dquery, base, offs):
    idx = unstriped(offs)
    keysu = unpack_weight(keys_words, keys_scales, "e2m1")
    valsu = unpack_weight(vals_words, vals_scales, "e2m1")
    queryq = mxq(f64(query), 0, "e4m3")
    keysidxg = keysu[:, idx]
    a = queryq.T @ keysidxg
    dqueryq = mxq(f64(dquery), 0, "e4m3")
    ta = dqueryq.T @ keysidxg
    p = np.exp(a - np.max(a, axis=1, keepdims=True))
    goutq = mxq(f64(gout), 0, "e4m3")
    valsidxg = valsu[:, idx]
    c0 = goutq.T @ valsidxg
    dpr = c0 * f64(mix)
    dpm = dpr.reshape(Q, G, I // G).sum(axis=2)
    e1 = dpm / 8.0
    r1 = np.repeat(e1, I // G, axis=1)
    dr = c0 * (1.0 - f64(mix)) + r1
    dp = dr / np.sum(p, axis=1, keepdims=True) + np.sum(dr * p / np.square(np.sum(p, axis=1, keepdims=True)) * (-1.0), axis=1, keepdims=True)
    tp = ta * p
    tdp = np.sum(tp, axis=1, keepdims=True) * dr / np.square(np.sum(p, axis=1, keepdims=True)) * (-1.0) + np.sum((tp * dr - np.sum(tp, axis=1, keepdims=True) * np.sum(p, axis=1, keepdims=True) * 2.0 * dr * p / np.square(np.sum(p, axis=1, keepdims=True))) / np.square(np.sum(p, axis=1, keepdims=True)) * (-1.0), axis=1, keepdims=True)
    tda = tdp * p + tp * dp
    gs = tda * 512.0
    gf = np.zeros((Q, T))
    gf[:, idx] = gs
    y = f64(base) + gf
    return y

@@ -1,0 +1,166 @@
+from contextlib import ExitStack
+
+import concourse.mybir as mybir
+
+F32 = mybir.dt.float32
+BF16 = mybir.dt.bfloat16
+I32 = mybir.dt.int32
+U32 = mybir.dt.uint32
+U16 = mybir.dt.uint16
+U8 = mybir.dt.uint8
+FP8X4 = mybir.dt.float8_e4m3fn_x4
+FP4X4 = mybir.dt.float4_e2m1fn_x4
+ALU = mybir.AluOpType
+ACT = mybir.ActivationFunctionType
+AX = mybir.AxisListType
+
+P = 128
+PACK = 4
+K = 512
+TOKENS = 2048
+SLOTS = 512
+ROWS = 128
+RUN = 8
+RUNS = SLOTS // RUN
+GAIN = 512.0
+STORE_COLS = (256, 512, 512, 512, 256)
+
+FLOPS = 3 * 2 * K * ROWS * SLOTS
+
+
+def tile_attend_hvdirect_smoothpage_s_kernel(
+    tc, query, keys_words, keys_scales, mix, gout, vals_words, vals_scales, dquery, base, offs, out
+):
+    nc = tc.nc
+    with ExitStack() as ctx:
+        sb = ctx.enter_context(tc.tile_pool(name="sb", bufs=1))
+        ps = ctx.enter_context(tc.psum_pool(name="ps", bufs=1))
+
+        def tile(name, cols, dtype, tag=""):
+            return sb.tile([P, cols], dtype, name=name, tag=tag or name, align_bytes=64)
+
+        def load_words(name, words):
+            pool_words = tile(name, TOKENS, U16)
+            nc.sync.dma_start(pool_words[:].bitcast(I32), words[0].bitcast(I32))
+            return pool_words
+
+        def load_scales(name, scales, clear):
+            plane = tile(name, TOKENS, U8)
+            clear.memset(plane[:].bitcast(I32), 0)
+            rows = scales[0].bitcast(I32)
+            for r in range(4):
+                nc.sync.dma_start(plane[r:P:32, :].bitcast(I32), rows[r:16:4, :])
+            return plane
+
+        def load_rows(name, rows, tag):
+            raw = sb.tile([P, PACK, ROWS], F32, name=name, tag=tag, align_bytes=64)
+            nc.sync.dma_start(raw[:], rows.rearrange("(p j) q -> p j q", j=PACK))
+            return raw
+
+        def gather(name, window, dtype):
+            picked = tile(name, SLOTS, dtype)
+            nc.vector.tensor_copy(picked[:], window[:].indirect(offsets[:]))
+            return picked
+
+        def quantise(name, raw):
+            woven = sb.tile([P, ROWS, PACK], BF16, name=name + "_bf", align_bytes=64)
+            nc.scalar.activation(
+                woven[:].rearrange("p (c i) j -> p c j i", i=4),
+                raw[:].rearrange("p j (c i) -> p c j i", i=4),
+                ACT.Copy,
+            )
+            codes = tile(name + "_codes", ROWS, U32)
+            scales = tile(name + "_scales", ROWS, U8)
+            nc.vector.quantize_mx(
+                out=codes[:].bitcast(FP8X4), scales=scales[:], in_=woven[:].rearrange("p q j -> p (q j)")
+            )
+            return codes, scales
+
+        def product(name, rows, words, scales):
+            acc = ps.tile([P, SLOTS], F32, name=name)
+            nc.tensor.matmul_mx(
+                out=acc[:],
+                lhsT=rows[0][:].bitcast(FP8X4),
+                lhsT_scale=rows[1][:],
+                rhs=words[:].bitcast(U8).bitcast(FP4X4),
+                rhs_scale=scales[:],
+                start=True,
+                stop=True,
+            )
+            return acc
+
+        offsets = sb.tile([P, SLOTS // 16], U16, name="offsets")
+        nc.sync.dma_start(offsets[:], offs)
+        val_words = load_words("val_words", vals_words)
+        key_words = load_words("key_words", keys_words)
+        gout_raw = load_rows("gout_raw", gout, "gout_raw")
+        query_raw = load_rows("query_raw", query, "query_raw")
+        val_scales = load_scales("val_scales", vals_scales, nc.vector)
+        dquery_raw = load_rows("dquery_raw", dquery, "dquery_raw")
+        key_scales = load_scales("key_scales", keys_scales, nc.vector)
+        mix_col = tile("mix_col", 1, F32)
+        nc.sync.dma_start(mix_col[:], mix)
+        placed = tile("placed", TOKENS, F32)
+        nc.vector.memset(placed[:], 0.0)
+
+        vw = gather("vw", val_words, U16)
+        kw = gather("kw", key_words, U16)
+        gout_mx = quantise("gout", gout_raw)
+        vs = gather("vs", val_scales, U8)
+        c0 = product("c0", gout_mx, vw, vs)
+        base_sb = tile("base_sb", TOKENS, F32, "val_scales")
+        nc.sync.dma_start(base_sb[:], base)
+        query_mx = quantise("query", query_raw)
+        dquery_mx = quantise("dquery", dquery_raw)
+        ks = gather("ks", key_scales, U8)
+        a = product("a", query_mx, kw, ks)
+        ta = product("ta", dquery_mx, kw, ks)
+        own = tile("own", 1, F32)
+        nc.scalar.activation(own[:], mix_col[:], ACT.Copy, scale=-GAIN, bias=GAIN)
+        shared = tile("shared", 1, F32)
+        nc.scalar.activation(shared[:], mix_col[:], ACT.Copy, scale=GAIN / RUN)
+
+        run_sum = tile("run_sum", RUNS, F32, "key_scales")
+        nc.vector.tensor_reduce(run_sum[:], c0[:].rearrange("p (g j) -> p g j", j=RUN), AX.X, ALU.add)
+        neg_max = tile("neg_max", 1, F32)
+        nc.vector.tensor_reduce(neg_max[:], a[:], AX.X, ALU.max, negate=True)
+        p = tile("p", SLOTS, F32)
+        p_sum = tile("p_sum", 1, F32)
+        nc.scalar.activation(p[:], a[:], ACT.Exp, bias=neg_max[:], accum_out=p_sum[:])
+        run_term = tile("run_term", RUNS, F32)
+        nc.vector.tensor_scalar(run_term[:], run_sum[:], shared[:], None, ALU.mult)
+        dr = tile("dr", SLOTS, F32)
+        nc.vector.scalar_tensor_tensor(
+            dr[:].rearrange("p (g j) -> p g j", j=RUN),
+            c0[:].rearrange("p (g j) -> p g j", j=RUN),
+            own[:],
+            run_term[:].unsqueeze(2).to_broadcast([P, RUNS, RUN]),
+            ALU.mult,
+            ALU.add,
+        )
+        inv = tile("inv", 1, F32)
+        nc.vector.reciprocal(inv[:], p_sum[:])
+        s = tile("s", SLOTS, F32)
+        nc.scalar.activation(s[:], p[:], ACT.Copy, scale=inv[:])
+        ta_s = tile("ta_s", SLOTS, F32)
+        ta_mean = tile("ta_mean", 1, F32)
+        nc.vector.scalar_tensor_tensor(ta_s[:], ta[:], inv[:], p[:], ALU.mult, ALU.mult, accum_out=ta_mean[:])
+        dr_s = tile("dr_s", SLOTS, F32)
+        dr_mean = tile("dr_mean", 1, F32)
+        nc.vector.scalar_tensor_tensor(dr_s[:], dr[:], inv[:], p[:], ALU.mult, ALU.mult, accum_out=dr_mean[:])
+        u = tile("u", SLOTS, F32)
+        nc.vector.scalar_tensor_tensor(u[:], ta[:], ta_mean[:], s[:], ALU.subtract, ALU.mult)
+        x = tile("x", SLOTS, F32)
+        cov = tile("cov", 1, F32)
+        nc.vector.scalar_tensor_tensor(x[:], dr[:], dr_mean[:], u[:], ALU.subtract, ALU.mult, accum_out=cov[:])
+        y = tile("y", SLOTS, F32)
+        nc.vector.tensor_scalar(y[:], s[:], cov[:], -1.0, ALU.mult, ALU.mult)
+        nc.vector.tensor_tensor(placed[:].indirect(offsets[:]), x[:], y[:], ALU.add)
+
+        start = 0
+        for n, cols in enumerate(STORE_COLS):
+            span = slice(start, start + cols)
+            total = tile("total%d" % n, cols, F32)
+            nc.vector.tensor_tensor(total[:], placed[:, span], base_sb[:, span], ALU.add)
+            nc.sync.dma_start(out[:, span], total[:])
+            start = start + cols

@@ -34,19 +34,24 @@ def tile_attend_hvdirect_smoothpage_s_kernel(
     nc = tc.nc
     with ExitStack() as ctx:
         sb = ctx.enter_context(tc.tile_pool(name="sb", bufs=1))
+        reuse = ctx.enter_context(tc.tile_pool(name="reuse", bufs=1))
         ps = ctx.enter_context(tc.psum_pool(name="ps", bufs=1))
 
         def tile(name, cols, dtype, tag=""):
             return sb.tile([P, cols], dtype, name=name, tag=tag or name, align_bytes=64)
 
-        def load_words(name, words):
-            pool_words = tile(name, TOKENS, U16)
+        def over_val_words(name, cols, dtype, offset):
+            return reuse.tile([P, cols], dtype, name=name, align_bytes=64, offset=offset)
+
+        def load_words(pool_words, words):
             nc.sync.dma_start(pool_words[:].bitcast(I32), words[0].bitcast(I32))
             return pool_words
 
-        def load_scales(name, scales, clear):
+        def load_scales(name, scales, engines):
             plane = tile(name, TOKENS, U8)
-            clear.memset(plane[:].bitcast(I32), 0)
+            share = TOKENS // len(engines)
+            for n, engine in enumerate(engines):
+                engine.memset(plane[:, n * share : (n + 1) * share].bitcast(I32), 0)
             rows = scales[0].bitcast(I32)
             for r in range(4):
                 nc.sync.dma_start(plane[r:P:32, :].bitcast(I32), rows[r:16:4, :])
@@ -62,14 +67,13 @@ def tile_attend_hvdirect_smoothpage_s_kernel(
             nc.vector.tensor_copy(picked[:], window[:].indirect(offsets[:]))
             return picked
 
-        def quantise(name, raw):
+        def quantise(name, raw, codes):
             woven = sb.tile([P, ROWS, PACK], BF16, name=name + "_bf", align_bytes=64)
             nc.scalar.activation(
                 woven[:].rearrange("p (c i) j -> p c j i", i=4),
                 raw[:].rearrange("p j (c i) -> p c j i", i=4),
                 ACT.Copy,
             )
-            codes = tile(name + "_codes", ROWS, U32)
             scales = tile(name + "_scales", ROWS, U8)
             nc.vector.quantize_mx(
                 out=codes[:].bitcast(FP8X4), scales=scales[:], in_=woven[:].rearrange("p q j -> p (q j)")
@@ -89,72 +93,74 @@ def tile_attend_hvdirect_smoothpage_s_kernel(
             )
             return acc
 
+        key_words = load_words(tile("key_words", TOKENS, U16), keys_words)
         offsets = sb.tile([P, SLOTS // 16], U16, name="offsets")
         nc.sync.dma_start(offsets[:], offs)
-        val_words = load_words("val_words", vals_words)
-        key_words = load_words("key_words", keys_words)
-        gout_raw = load_rows("gout_raw", gout, "gout_raw")
         query_raw = load_rows("query_raw", query, "query_raw")
-        val_scales = load_scales("val_scales", vals_scales, nc.vector)
-        dquery_raw = load_rows("dquery_raw", dquery, "dquery_raw")
-        key_scales = load_scales("key_scales", keys_scales, nc.vector)
         mix_col = tile("mix_col", 1, F32)
         nc.sync.dma_start(mix_col[:], mix)
+        val_scales = load_scales("val_scales", vals_scales, (nc.vector, nc.gpsimd))
+        dquery_raw = load_rows("dquery_raw", dquery, "dquery_raw")
+        key_scales = load_scales("key_scales", keys_scales, (nc.gpsimd,))
+        gout_raw = load_rows("gout_raw", gout, "gout_raw")
+        val_words = load_words(over_val_words("val_words", TOKENS, U16, 0), vals_words)
         placed = tile("placed", TOKENS, F32)
         nc.vector.memset(placed[:], 0.0)
 
-        vw = gather("vw", val_words, U16)
         kw = gather("kw", key_words, U16)
-        gout_mx = quantise("gout", gout_raw)
+        query_mx = quantise("query", query_raw, tile("query_codes", ROWS, U32))
         vs = gather("vs", val_scales, U8)
-        c0 = product("c0", gout_mx, vw, vs)
-        base_sb = tile("base_sb", TOKENS, F32, "val_scales")
-        nc.sync.dma_start(base_sb[:], base)
-        query_mx = quantise("query", query_raw)
-        dquery_mx = quantise("dquery", dquery_raw)
         ks = gather("ks", key_scales, U8)
         a = product("a", query_mx, kw, ks)
-        ta = product("ta", dquery_mx, kw, ks)
+        base_sb = tile("base_sb", TOKENS, F32, "key_scales")
+        nc.sync.dma_start(base_sb[:], base)
         own = tile("own", 1, F32)
         nc.scalar.activation(own[:], mix_col[:], ACT.Copy, scale=-GAIN, bias=GAIN)
         shared = tile("shared", 1, F32)
         nc.scalar.activation(shared[:], mix_col[:], ACT.Copy, scale=GAIN / RUN)
-
-        run_sum = tile("run_sum", RUNS, F32, "key_scales")
-        nc.vector.tensor_reduce(run_sum[:], c0[:].rearrange("p (g j) -> p g j", j=RUN), AX.X, ALU.add)
-        neg_max = tile("neg_max", 1, F32)
+        gout_mx = quantise("gout", gout_raw, tile("gout_codes", ROWS, U32))
+        vw = gather("vw", val_words, U16)
+        c0 = product("c0", gout_mx, vw, vs)
+        neg_max = over_val_words("neg_max", 1, F32, 0)
         nc.vector.tensor_reduce(neg_max[:], a[:], AX.X, ALU.max, negate=True)
+        dquery_mx = quantise("dquery", dquery_raw, over_val_words("dquery_codes", ROWS, U32, 64))
+        ta = product("ta", dquery_mx, kw, ks)
         p = tile("p", SLOTS, F32)
         p_sum = tile("p_sum", 1, F32)
         nc.scalar.activation(p[:], a[:], ACT.Exp, bias=neg_max[:], accum_out=p_sum[:])
+
+        run_sum = tile("run_sum", RUNS, F32)
+        nc.vector.tensor_reduce(run_sum[:], c0[:].rearrange("p (g j) -> p g j", j=RUN), AX.X, ALU.add)
+        inv = tile("inv", 1, F32)
+        nc.vector.reciprocal(inv[:], p_sum[:])
+        own_n = tile("own_n", 1, F32)
+        nc.scalar.activation(own_n[:], own[:], ACT.Copy, scale=inv[:])
+        neg_inv = tile("neg_inv", 1, F32)
+        nc.scalar.activation(neg_inv[:], inv[:], ACT.Copy, scale=-1.0)
         run_term = tile("run_term", RUNS, F32)
-        nc.vector.tensor_scalar(run_term[:], run_sum[:], shared[:], None, ALU.mult)
+        nc.vector.tensor_scalar(run_term[:], run_sum[:], shared[:], inv[:], ALU.mult, ALU.mult)
+        ta_s = tile("ta_s", SLOTS, F32)
+        ta_mean = tile("ta_mean", 1, F32)
+        nc.vector.scalar_tensor_tensor(ta_s[:], ta[:], inv[:], p[:], ALU.mult, ALU.mult, accum_out=ta_mean[:])
         dr = tile("dr", SLOTS, F32)
         nc.vector.scalar_tensor_tensor(
             dr[:].rearrange("p (g j) -> p g j", j=RUN),
             c0[:].rearrange("p (g j) -> p g j", j=RUN),
-            own[:],
+            own_n[:],
             run_term[:].unsqueeze(2).to_broadcast([P, RUNS, RUN]),
             ALU.mult,
             ALU.add,
         )
-        inv = tile("inv", 1, F32)
-        nc.vector.reciprocal(inv[:], p_sum[:])
-        s = tile("s", SLOTS, F32)
-        nc.scalar.activation(s[:], p[:], ACT.Copy, scale=inv[:])
-        ta_s = tile("ta_s", SLOTS, F32)
-        ta_mean = tile("ta_mean", 1, F32)
-        nc.vector.scalar_tensor_tensor(ta_s[:], ta[:], inv[:], p[:], ALU.mult, ALU.mult, accum_out=ta_mean[:])
+        u = tile("u", SLOTS, F32)
+        nc.vector.scalar_tensor_tensor(u[:], ta[:], ta_mean[:], p[:], ALU.subtract, ALU.mult)
         dr_s = tile("dr_s", SLOTS, F32)
         dr_mean = tile("dr_mean", 1, F32)
         nc.vector.scalar_tensor_tensor(dr_s[:], dr[:], inv[:], p[:], ALU.mult, ALU.mult, accum_out=dr_mean[:])
-        u = tile("u", SLOTS, F32)
-        nc.vector.scalar_tensor_tensor(u[:], ta[:], ta_mean[:], s[:], ALU.subtract, ALU.mult)
         x = tile("x", SLOTS, F32)
         cov = tile("cov", 1, F32)
         nc.vector.scalar_tensor_tensor(x[:], dr[:], dr_mean[:], u[:], ALU.subtract, ALU.mult, accum_out=cov[:])
         y = tile("y", SLOTS, F32)
-        nc.vector.tensor_scalar(y[:], s[:], cov[:], -1.0, ALU.mult, ALU.mult)
+        nc.vector.tensor_scalar(y[:], p[:], cov[:], neg_inv[:], ALU.mult, ALU.mult)
         nc.vector.tensor_tensor(placed[:].indirect(offsets[:]), x[:], y[:], ALU.add)
 
         start = 0

@@ -23,7 +23,7 @@ ROWS = 128
 RUN = 8
 RUNS = SLOTS // RUN
 GAIN = 512.0
-STORE_COLS = (256, 512, 512, 512, 256)
+STORE_COLS = (128, 384, 512, 512, 384, 128)
 
 FLOPS = 3 * 2 * K * ROWS * SLOTS
 
@@ -100,10 +100,10 @@ def tile_attend_hvdirect_smoothpage_s_kernel(
         mix_col = tile("mix_col", 1, F32)
         nc.sync.dma_start(mix_col[:], mix)
         val_scales = load_scales("val_scales", vals_scales, (nc.vector, nc.gpsimd))
-        dquery_raw = load_rows("dquery_raw", dquery, "dquery_raw")
         key_scales = load_scales("key_scales", keys_scales, (nc.gpsimd,))
         gout_raw = load_rows("gout_raw", gout, "gout_raw")
         val_words = load_words(over_val_words("val_words", TOKENS, U16, 0), vals_words)
+        dquery_raw = load_rows("dquery_raw", dquery, "dquery_raw")
         placed = tile("placed", TOKENS, F32)
         nc.vector.memset(placed[:], 0.0)
 
@@ -129,7 +129,7 @@ def tile_attend_hvdirect_smoothpage_s_kernel(
         p_sum = tile("p_sum", 1, F32)
         nc.scalar.activation(p[:], a[:], ACT.Exp, bias=neg_max[:], accum_out=p_sum[:])
 
-        run_sum = tile("run_sum", RUNS, F32)
+        run_sum = tile("run_sum", RUNS, F32, "dquery_bf")
         nc.vector.tensor_reduce(run_sum[:], c0[:].rearrange("p (g j) -> p g j", j=RUN), AX.X, ALU.add)
         inv = tile("inv", 1, F32)
         nc.vector.reciprocal(inv[:], p_sum[:])

from contextlib import ExitStack

import concourse.mybir as mybir

F32 = mybir.dt.float32
BF16 = mybir.dt.bfloat16
I32 = mybir.dt.int32
U32 = mybir.dt.uint32
U16 = mybir.dt.uint16
U8 = mybir.dt.uint8
FP8X4 = mybir.dt.float8_e4m3fn_x4
FP4X4 = mybir.dt.float4_e2m1fn_x4
ALU = mybir.AluOpType
ACT = mybir.ActivationFunctionType
AX = mybir.AxisListType

P = 128
PACK = 4
K = 512
TOKENS = 2048
SLOTS = 512
ROWS = 128
RUN = 8
RUNS = SLOTS // RUN
GAIN = 512.0
STORE_COLS = (128, 384, 512, 512, 384, 128)

FLOPS = 3 * 2 * K * ROWS * SLOTS


def tile_attend_hvdirect_smoothpage_s_kernel(
    tc, query, keys_words, keys_scales, mix, gout, vals_words, vals_scales, dquery, base, offs, out
):
    nc = tc.nc
    with ExitStack() as ctx:
        sb = ctx.enter_context(tc.tile_pool(name="sb", bufs=1))
        reuse = ctx.enter_context(tc.tile_pool(name="reuse", bufs=1))
        ps = ctx.enter_context(tc.psum_pool(name="ps", bufs=1))

        def tile(name, cols, dtype, tag=""):
            return sb.tile([P, cols], dtype, name=name, tag=tag or name, align_bytes=64)

        def over_val_words(name, cols, dtype, offset):
            return reuse.tile([P, cols], dtype, name=name, align_bytes=64, offset=offset)

        def load_words(pool_words, words):
            nc.sync.dma_start(pool_words[:].bitcast(I32), words[0].bitcast(I32))
            return pool_words

        def load_scales(name, scales, engines):
            plane = tile(name, TOKENS, U8)
            share = TOKENS // len(engines)
            for n, engine in enumerate(engines):
                engine.memset(plane[:, n * share : (n + 1) * share].bitcast(I32), 0)
            rows = scales[0].bitcast(I32)
            for r in range(4):
                nc.sync.dma_start(plane[r:P:32, :].bitcast(I32), rows[r:16:4, :])
            return plane

        def load_rows(name, rows, tag):
            raw = sb.tile([P, PACK, ROWS], F32, name=name, tag=tag, align_bytes=64)
            nc.sync.dma_start(raw[:], rows.rearrange("(p j) q -> p j q", j=PACK))
            return raw

        def gather(name, window, dtype):
            picked = tile(name, SLOTS, dtype)
            nc.vector.tensor_copy(picked[:], window[:].indirect(offsets[:]))
            return picked

        def quantise(name, raw, codes):
            woven = sb.tile([P, ROWS, PACK], BF16, name=name + "_bf", align_bytes=64)
            nc.scalar.activation(
                woven[:].rearrange("p (c i) j -> p c j i", i=4),
                raw[:].rearrange("p j (c i) -> p c j i", i=4),
                ACT.Copy,
            )
            scales = tile(name + "_scales", ROWS, U8)
            nc.vector.quantize_mx(
                out=codes[:].bitcast(FP8X4), scales=scales[:], in_=woven[:].rearrange("p q j -> p (q j)")
            )
            return codes, scales

        def product(name, rows, words, scales):
            acc = ps.tile([P, SLOTS], F32, name=name)
            nc.tensor.matmul_mx(
                out=acc[:],
                lhsT=rows[0][:].bitcast(FP8X4),
                lhsT_scale=rows[1][:],
                rhs=words[:].bitcast(U8).bitcast(FP4X4),
                rhs_scale=scales[:],
                start=True,
                stop=True,
            )
            return acc

        key_words = load_words(tile("key_words", TOKENS, U16), keys_words)
        offsets = sb.tile([P, SLOTS // 16], U16, name="offsets")
        nc.sync.dma_start(offsets[:], offs)
        query_raw = load_rows("query_raw", query, "query_raw")
        mix_col = tile("mix_col", 1, F32)
        nc.sync.dma_start(mix_col[:], mix)
        val_scales = load_scales("val_scales", vals_scales, (nc.vector, nc.gpsimd))
        key_scales = load_scales("key_scales", keys_scales, (nc.gpsimd,))
        gout_raw = load_rows("gout_raw", gout, "gout_raw")
        val_words = load_words(over_val_words("val_words", TOKENS, U16, 0), vals_words)
        dquery_raw = load_rows("dquery_raw", dquery, "dquery_raw")
        placed = tile("placed", TOKENS, F32)
        nc.vector.memset(placed[:], 0.0)

        kw = gather("kw", key_words, U16)
        query_mx = quantise("query", query_raw, tile("query_codes", ROWS, U32))
        vs = gather("vs", val_scales, U8)
        ks = gather("ks", key_scales, U8)
        a = product("a", query_mx, kw, ks)
        base_sb = tile("base_sb", TOKENS, F32, "key_scales")
        nc.sync.dma_start(base_sb[:], base)
        own = tile("own", 1, F32)
        nc.scalar.activation(own[:], mix_col[:], ACT.Copy, scale=-GAIN, bias=GAIN)
        shared = tile("shared", 1, F32)
        nc.scalar.activation(shared[:], mix_col[:], ACT.Copy, scale=GAIN / RUN)
        gout_mx = quantise("gout", gout_raw, tile("gout_codes", ROWS, U32))
        vw = gather("vw", val_words, U16)
        c0 = product("c0", gout_mx, vw, vs)
        neg_max = over_val_words("neg_max", 1, F32, 0)
        nc.vector.tensor_reduce(neg_max[:], a[:], AX.X, ALU.max, negate=True)
        dquery_mx = quantise("dquery", dquery_raw, over_val_words("dquery_codes", ROWS, U32, 64))
        ta = product("ta", dquery_mx, kw, ks)
        p = tile("p", SLOTS, F32)
        p_sum = tile("p_sum", 1, F32)
        nc.scalar.activation(p[:], a[:], ACT.Exp, bias=neg_max[:], accum_out=p_sum[:])

        run_sum = tile("run_sum", RUNS, F32, "dquery_bf")
        nc.vector.tensor_reduce(run_sum[:], c0[:].rearrange("p (g j) -> p g j", j=RUN), AX.X, ALU.add)
        inv = tile("inv", 1, F32)
        nc.vector.reciprocal(inv[:], p_sum[:])
        own_n = tile("own_n", 1, F32)
        nc.scalar.activation(own_n[:], own[:], ACT.Copy, scale=inv[:])
        neg_inv = tile("neg_inv", 1, F32)
        nc.scalar.activation(neg_inv[:], inv[:], ACT.Copy, scale=-1.0)
        run_term = tile("run_term", RUNS, F32)
        nc.vector.tensor_scalar(run_term[:], run_sum[:], shared[:], inv[:], ALU.mult, ALU.mult)
        ta_s = tile("ta_s", SLOTS, F32)
        ta_mean = tile("ta_mean", 1, F32)
        nc.vector.scalar_tensor_tensor(ta_s[:], ta[:], inv[:], p[:], ALU.mult, ALU.mult, accum_out=ta_mean[:])
        dr = tile("dr", SLOTS, F32)
        nc.vector.scalar_tensor_tensor(
            dr[:].rearrange("p (g j) -> p g j", j=RUN),
            c0[:].rearrange("p (g j) -> p g j", j=RUN),
            own_n[:],
            run_term[:].unsqueeze(2).to_broadcast([P, RUNS, RUN]),
            ALU.mult,
            ALU.add,
        )
        u = tile("u", SLOTS, F32)
        nc.vector.scalar_tensor_tensor(u[:], ta[:], ta_mean[:], p[:], ALU.subtract, ALU.mult)
        dr_s = tile("dr_s", SLOTS, F32)
        dr_mean = tile("dr_mean", 1, F32)
        nc.vector.scalar_tensor_tensor(dr_s[:], dr[:], inv[:], p[:], ALU.mult, ALU.mult, accum_out=dr_mean[:])
        x = tile("x", SLOTS, F32)
        cov = tile("cov", 1, F32)
        nc.vector.scalar_tensor_tensor(x[:], dr[:], dr_mean[:], u[:], ALU.subtract, ALU.mult, accum_out=cov[:])
        y = tile("y", SLOTS, F32)
        nc.vector.tensor_scalar(y[:], p[:], cov[:], neg_inv[:], ALU.mult, ALU.mult)
        nc.vector.tensor_tensor(placed[:].indirect(offsets[:]), x[:], y[:], ALU.add)

        start = 0
        for n, cols in enumerate(STORE_COLS):
            span = slice(start, start + cols)
            total = tile("total%d" % n, cols, F32)
            nc.vector.tensor_tensor(total[:], placed[:, span], base_sb[:, span], ALU.add)
            nc.sync.dma_start(out[:, span], total[:])
            start = start + cols
